import numpy as np
import ml_dtypes


def mxq(x, axis, fmt="e4m3"):
    dtype, down = {"e4m3": (ml_dtypes.float8_e4m3fn, 7), "e5m2": (ml_dtypes.float8_e5m2, 14)}[fmt]
    v = np.moveaxis(np.asarray(x, np.float32).astype(ml_dtypes.bfloat16).astype(np.float64), axis, -1)
    blocks = v.reshape(v.shape[:-1] + (-1, 32))
    amax = np.abs(blocks).max(-1, keepdims=True)
    byte = np.maximum(np.where(amax > 0, np.frexp(amax)[1] - 1 + 127, 0) - down, 1)
    scale = np.exp2(byte - 127.0)
    codes = (blocks / scale).astype(np.float32).astype(dtype).astype(np.float64)
    return np.moveaxis((codes * scale).reshape(v.shape), -1, axis)


WIDE = False


def mx_kscale(k):
    if not WIDE:
        return np.ones(k)
    levels = np.array([30, -30])
    if k % 512:
        return np.exp2(np.random.permutation(np.resize(levels, k // 32))).repeat(32)
    a = np.empty((k // 512, 16))
    for p in range(k // 512):
        a[p, :8] = np.random.permutation(np.resize(levels, 8))
        for g in range(8):
            far = levels[np.abs(levels - a[p, g]) >= 10]
            a[p, g + 8] = far[np.random.randint(len(far))]
    return np.exp2(a.ravel()).repeat(32)


def f64(x):
    return np.asarray(x).astype(np.float64)


def striped(idx):
    return np.tile(np.asarray(idx).reshape(-1, 16).T, (8, 1)).astype(np.uint16)


def unstriped(offs):
    return offs[:16].T.reshape(-1).astype(np.int64)


E2M1 = np.array([0.0, 0.5, 1.0, 1.5, 2.0, 3.0, 4.0, 6.0, -0.0, -0.5, -1.0, -1.5, -2.0, -3.0, -4.0, -6.0])


def pack_weight(w, fmt):
    k, n = w.shape
    w = f64(np.asarray(w, np.float32).astype(ml_dtypes.bfloat16)).reshape(k // 32, 32, n)
    amax = np.abs(w).max(1)
    if fmt in ("e4m3", "e5m2"):
        byte = np.frexp(amax)[1] - 1 + 127 - (7 if fmt == "e4m3" else 14)
    else:
        mant, ex = np.frexp(amax / 6.0)
        byte = np.where(mant > 0.5, ex, ex - 1) + 127
    byte = np.clip(np.where(amax > 0, byte, 1), 1, 254)
    scaled = (w * np.exp2(127.0 - byte)[:, None, :]).reshape(k, n).astype(np.float32)
    by_word = np.ascontiguousarray(scaled.reshape(k // 512, 128, 4, n).transpose(0, 1, 3, 2))
    if fmt in ("e4m3", "e5m2"):
        words = by_word.astype(ml_dtypes.float8_e4m3fn if fmt == "e4m3" else ml_dtypes.float8_e5m2).view(np.uint8)
    else:
        c = by_word.astype(ml_dtypes.float4_e2m1fn).view(np.uint8) & 0xF
        words = (c[..., 0::2] | (c[..., 1::2] << 4)).reshape(k // 512, 128, 2 * n)
    return np.ascontiguousarray(words), np.ascontiguousarray(byte.astype(np.uint8).reshape(k // 512, 16, n))


def unpack_weight(words, scales, fmt):
    g, _, n = scales.shape
    words = np.ascontiguousarray(words).reshape(g, 128, n, -1)
    if fmt in ("e4m3", "e5m2"):
        vals = words.view(ml_dtypes.float8_e4m3fn if fmt == "e4m3" else ml_dtypes.float8_e5m2).astype(np.float64)
    else:
        nib = np.empty((g, 128, n, 4), np.uint8)
        nib[..., 0::2] = words & 0xF
        nib[..., 1::2] = words >> 4
        vals = E2M1[nib]
    vals = vals * np.repeat(np.exp2(scales.astype(np.float64) - 127.0), 8, axis=1)[..., None]
    return vals.transpose(0, 1, 3, 2).reshape(g * 512, n)


def sigmoid(v):
    return 1.0 / (1.0 + np.exp(-v))


K, T, Z, J, R, C, O, N, E = 512, 1024, 1024, 256, 512, 512, 256, 256, 1024


def setup_inputs():
    n = np.random.standard_normal
    idx = np.random.permutation(T)[:J]
    idx2 = np.random.permutation(Z)[:J]
    idx3 = np.random.permutation(C)[:J]
    idx4 = np.random.permutation(C)[:J]
    idx5 = np.random.permutation(C)[:O]
    idx6 = np.random.permutation(E)[:O]
    fk = mx_kscale(K)
    fr = mx_kscale(R)
    xtp = pack_weight(n((K, T)) / fk[:, None], "e2m1")
    xop = pack_weight(n((K, Z)) / fk[:, None], "e4m3")
    wp = pack_weight(n((K, R)) * 1 / np.sqrt(K) * fk[:, None] * fr, "e4m3")
    w2p = pack_weight(n((K, R)) * 1 / np.sqrt(K) * fk[:, None] * fr, "e5m2")
    wbp = pack_weight(n((R, N)) * 1 / np.sqrt(R) / fr[:, None], "e2m1")
    return {
        "xt_words": xtp[0],
        "xt_scales": xtp[1],
        "xo_words": xop[0],
        "xo_scales": xop[1],
        "w_words": wp[0],
        "w_scales": wp[1],
        "w2_words": w2p[0],
        "w2_scales": w2p[1],
        "wb_words": wbp[0],
        "wb_scales": wbp[1],
        "tz": (n((N, E))).astype(np.float32),
        "so": (np.random.uniform(0.6, 1.6, (N, 1))).astype(np.float32),
        "bo": (np.random.uniform(-1.0, 1.0, (N, 1))).astype(np.float32),
        "offs": striped(idx),
        "offs2": striped(idx2),
        "offs3": striped(idx3),
        "offs4": striped(idx4),
        "offs5": striped(idx5),
        "offs6": striped(idx6),
    }


def reference(xt_words, xt_scales, xo_words, xo_scales, w_words, w_scales, w2_words, w2_scales, wb_words, wb_scales, tz, so, bo, offs, offs2, offs3, offs4, offs5, offs6):
    idx = unstriped(offs)
    idx2 = unstriped(offs2)
    idx3 = unstriped(offs3)
    idx4 = unstriped(offs4)
    idx5 = unstriped(offs5)
    idx6 = unstriped(offs6)
    xtu = unpack_weight(xt_words, xt_scales, "e2m1")
    xou = unpack_weight(xo_words, xo_scales, "e4m3")
    wu = unpack_weight(w_words, w_scales, "e4m3")
    w2u = unpack_weight(w2_words, w2_scales, "e5m2")
    wbu = unpack_weight(wb_words, wb_scales, "e2m1")
    xtidxg = xtu[:, idx]
    xoidx2g = xou[:, idx2]
    a = wu.T @ xtidxg + w2u.T @ xoidx2g
    b = w2u.T @ xtidxg + wu.T @ xoidx2g
    pw = np.zeros((R, C))
    pw[:, idx3] = a
    pv = np.zeros((R, C))
    pv[:, idx4] = b
    pg = pw + pv
    hid = pg[:, idx5]
    hidq = mxq(hid, 0, "e5m2")
    p = wbu.T @ hidq
    y = p * sigmoid(f64(tz)[:, idx6] * f64(so) + f64(bo))
    return y

@@ -1,0 +1,185 @@
+from contextlib import ExitStack
+
+import concourse.mybir as mybir
+
+F32 = mybir.dt.float32
+BF16 = mybir.dt.bfloat16
+I32 = mybir.dt.int32
+U32 = mybir.dt.uint32
+U16 = mybir.dt.uint16
+U8 = mybir.dt.uint8
+E4M3 = mybir.dt.float8_e4m3fn_x4
+E5M2 = mybir.dt.float8_e5m2_x4
+E2M1 = mybir.dt.float4_e2m1fn_x4
+ACT = mybir.ActivationFunctionType
+ALU = mybir.AluOpType
+
+K, T, Z, J, R, C, O, N, E = 512, 1024, 1024, 256, 512, 512, 256, 256, 1024
+P = 128
+PACK = 4
+FLOPS = 2 * (4 * K * R * J + R * N * O)
+
+
+def load_scale_rows(queue, plane, scales):
+    for q in range(4):
+        queue.dma_start(
+            out=plane[32 * q : 32 * q + 4, :].bitcast(I32),
+            in_=scales[0, 4 * q : 4 * q + 4, :].bitcast(I32),
+        )
+
+
+def tile_list_crossed_shared_one_finalgate_kernel(
+    tc, xt_words, xt_scales, xo_words, xo_scales, w_words, w_scales, w2_words, w2_scales,
+    wb_words, wb_scales, tz, so, bo, offs, offs2, offs3, offs4, offs5, offs6, out,
+):
+    nc = tc.nc
+    with ExitStack() as ctx:
+        lists = ctx.enter_context(tc.tile_pool(name="lists", bufs=1))
+        sb = ctx.enter_context(tc.tile_pool(name="sb", bufs=1))
+        ps = ctx.enter_context(tc.psum_pool(name="ps", bufs=1))
+
+        def new_list(name):
+            return lists.tile([P, J // 16], U16, name=name)
+
+        def new(shape, dtype, name, tag=None):
+            return sb.tile(shape, dtype, name=name, tag=tag or name, align_bytes=64)
+
+        l_xt, l_xo, l_a, l_b, l_hid, l_gate = [new_list("list%d" % i) for i in range(6)]
+
+        xt_sc = new([P, T], U8, "xt_sc")
+        xo_sc = new([P, Z], U8, "xo_sc")
+        w_sc_raw = new([P, R], U8, "w_sc_raw")
+        w2_sc_raw = new([P, R], U8, "w2_sc_raw")
+        nc.gpsimd.memset(w2_sc_raw[:].bitcast(I32), 0)
+        for plane in (xt_sc, xo_sc, w_sc_raw):
+            nc.vector.memset(plane[:].bitcast(I32), 0)
+
+        xt_tab = new([P, T], U16, "xt_tab")
+        xo_tab = new([P, Z], U32, "xo_tab")
+        w_raw = new([P, R], U32, "w_raw")
+        w2_raw = new([P, R], U32, "w2_raw")
+
+        nc.sync.dma_start(l_xt[:], offs)
+        nc.sync.dma_start(l_xo[:], offs2)
+        nc.sync.dma_start(out=xt_tab[:].bitcast(I32), in_=xt_words[0].bitcast(I32))
+        load_scale_rows(nc.sync, xt_sc, xt_scales)
+        nc.sync.dma_start(out=xo_tab[:].bitcast(I32), in_=xo_words[0].rearrange("p n t -> p (n t)").bitcast(I32))
+        load_scale_rows(nc.sync, xo_sc, xo_scales)
+        nc.sync.dma_start(out=w_raw[:].bitcast(I32), in_=w_words[0].rearrange("p n t -> p (n t)").bitcast(I32))
+        nc.sync.dma_start(out=w2_raw[:].bitcast(I32), in_=w2_words[0].rearrange("p n t -> p (n t)").bitcast(I32))
+        load_scale_rows(nc.sync, w_sc_raw, w_scales)
+        load_scale_rows(nc.gpsimd, w2_sc_raw, w2_scales)
+        nc.sync.dma_start(l_a[:], offs3)
+        nc.sync.dma_start(l_b[:], offs4)
+        nc.sync.dma_start(l_hid[:], offs5)
+        nc.sync.dma_start(l_gate[:], offs6)
+
+        pw = [new([P, C], F32, "pw%d" % t) for t in range(2)]
+        pv = [new([P, C], F32, "pv%d" % t) for t in range(2)]
+        for t in range(2):
+            nc.vector.memset(pw[t][:], 0.0)
+            nc.vector.memset(pv[t][:], 0.0)
+
+        xt_g = new([P, J], U16, "xt_g")
+        xt_gs = new([P, J], U8, "xt_gs")
+        xo_g = new([P, J], U32, "xo_g")
+        xo_gs = new([P, J], U8, "xo_gs")
+        w_codes = new([P, R], U32, "w_codes")
+        w2_codes = new([P, R], U32, "w2_codes")
+        w_sc = new([P, R], U8, "w_sc")
+        w2_sc = new([P, R], U8, "w2_sc")
+
+        nc.vector.tensor_copy(out=xt_g[:], in_=xt_tab[:].indirect(l_xt[:]))
+        nc.vector.tensor_copy(out=xt_gs[:], in_=xt_sc[:].indirect(l_xt[:]))
+        nc.vector.tensor_copy(out=xo_g[:], in_=xo_tab[:].indirect(l_xo[:]))
+        nc.vector.tensor_copy(out=xo_gs[:], in_=xo_sc[:].indirect(l_xo[:]))
+        for dst, raw in ((w_codes, w_raw), (w2_codes, w2_raw)):
+            nc.scalar.copy(
+                out=dst[:].rearrange("p (t g i) -> p g t i", t=PACK, i=4),
+                in_=raw[:].rearrange("p (g i t) -> p g t i", t=PACK, i=4),
+            )
+        for dst, raw in ((w_sc, w_sc_raw), (w2_sc, w2_sc_raw)):
+            nc.vector.tensor_copy(
+                out=dst[:].rearrange("p (t g i) -> p g t i", t=PACK, i=16),
+                in_=raw[:].rearrange("p (g i t) -> p g t i", t=PACK, i=16),
+            )
+
+        tz_tab = [new([P, E], F32, "tz%d" % h, tag) for h, tag in enumerate(("xt_tab", "xo_tab"))]
+        slope = new([P, 2], F32, "slope", "xt_sc")
+        offset = new([P, 2], F32, "offset", "xo_sc")
+        wb_codes = new([P, 2 * N], U8, "wb_codes", "w_raw")
+        wb_sc = new([P, N], U8, "wb_sc", "w2_sc_raw")
+        nc.gpsimd.memset(wb_sc[:].bitcast(I32), 0)
+        nc.sync.dma_start(out=wb_codes[:].bitcast(I32), in_=wb_words[0].bitcast(I32))
+        load_scale_rows(nc.sync, wb_sc, wb_scales)
+        for h in range(2):
+            nc.sync.dma_start(out=tz_tab[h][:], in_=tz[h * P : (h + 1) * P, :])
+        with nc.allow_non_contiguous_dma(reason="one slope and one offset a partition"):
+            nc.sync.dma_start(out=slope[:], in_=so.rearrange("(h p) o -> p (h o)", p=P))
+            nc.sync.dma_start(out=offset[:], in_=bo.rearrange("(h p) o -> p (h o)", p=P))
+
+        def product(acc, t, first, first_sc, first_fmt, second, second_sc, second_fmt):
+            cols = slice(t * P, (t + 1) * P)
+            nc.tensor.matmul_mx(
+                out=acc[:], lhsT=first[:, cols].bitcast(first_fmt), lhsT_scale=first_sc[:, cols],
+                rhs=xt_g[:].bitcast(E2M1), rhs_scale=xt_gs[:], start=True, stop=False,
+            )
+            nc.tensor.matmul_mx(
+                out=acc[:], lhsT=second[:, cols].bitcast(second_fmt), lhsT_scale=second_sc[:, cols],
+                rhs=xo_g[:].bitcast(E4M3), rhs_scale=xo_gs[:], start=False, stop=True,
+            )
+
+        hid_planes = new([P, PACK, O], BF16, "hid_planes")
+        half = O // 2
+        for t in range(PACK):
+            acc_a = ps.tile([P, J], F32, name="acc_a", tag="acc_a%d" % (t % 3))
+            acc_b = ps.tile([P, J], F32, name="acc_b", tag="acc_b%d" % (t % 3))
+            product(acc_a, t, w_codes, w_sc, E4M3, w2_codes, w2_sc, E5M2)
+            product(acc_b, t, w2_codes, w2_sc, E5M2, w_codes, w_sc, E4M3)
+            a_sb = sb.tile([P, J], F32, name="a_sb", tag="a_sb%d" % t, align_bytes=64)
+            b_sb = sb.tile([P, J], F32, name="b_sb", tag="b_sb%d" % t, align_bytes=64)
+            nc.scalar.copy(out=a_sb[:], in_=acc_a[:])
+            nc.vector.tensor_copy(out=b_sb[:], in_=acc_b[:])
+            nc.scalar.activation(out=pw[t % 2][:].indirect(l_a[:]), in_=a_sb[:], func=ACT.Copy)
+            nc.vector.tensor_copy(out=pv[t % 2][:].indirect(l_b[:]), in_=b_sb[:])
+            pg = sb.tile([P, C], F32, name="pg", tag="pg%d" % t, align_bytes=64)
+            nc.vector.tensor_tensor(out=pg[:], in0=pw[t % 2][:], in1=pv[t % 2][:], op=ALU.add)
+            if t < PACK - 1:
+                nc.scalar.activation(out=hid_planes[:, t, :], in_=pg[:].indirect(l_hid[:]), func=ACT.Copy)
+            else:
+                nc.vector.tensor_copy(out=hid_planes[:, t, 0:half], in_=pg[:].indirect(l_hid[:, 0:8]))
+                nc.scalar.activation(out=hid_planes[:, t, half:O], in_=pg[:].indirect(l_hid[:, 8:16]), func=ACT.Copy)
+
+        def make_gate(h, tag):
+            gate = sb.tile([P, O], F32, name="gate", tag=tag, align_bytes=64)
+            nc.scalar.activation(
+                out=gate[:], in_=tz_tab[h][:].indirect(l_gate[:]), func=ACT.Sigmoid,
+                bias=offset[:, h : h + 1], scale=slope[:, h : h + 1],
+            )
+            return gate
+
+        gates = [make_gate(0, "a_sb3")]
+
+        hid_words = [new([P, half * PACK], BF16, "hid_words%d" % u) for u in range(2)]
+        for u, copy in enumerate((nc.vector.tensor_copy, nc.scalar.copy)):
+            copy(
+                out=hid_words[u][:].rearrange("p (c i t) -> p c t i", t=PACK, i=4),
+                in_=hid_planes[:, :, u * half : (u + 1) * half].rearrange("p t (c i) -> p c t i", i=4),
+            )
+        gates.append(make_gate(1, "pg3"))
+        res = [new([P, O], F32, "res%d" % h) for h in range(2)]
+        for u in range(2):
+            cols = slice(u * half, (u + 1) * half)
+            hid_codes = new([P, half], U32, "hid_codes%d" % u)
+            hid_sc = new([P, half], U8, "hid_sc%d" % u)
+            nc.vector.quantize_mx(out=hid_codes[:].bitcast(E5M2), scales=hid_sc[:], in_=hid_words[u][:])
+            for h in range(2):
+                acc_p = ps.tile([P, half], F32, name="acc_p", tag=("acc_p0", "acc_p1", "acc_a1", "acc_b1")[2 * u + h])
+                nc.tensor.matmul_mx(
+                    out=acc_p[:], lhsT=wb_codes[:, 2 * h * P : 2 * (h + 1) * P].bitcast(E2M1),
+                    lhsT_scale=wb_sc[:, h * P : (h + 1) * P],
+                    rhs=hid_codes[:].bitcast(E5M2), rhs_scale=hid_sc[:], start=True, stop=True,
+                )
+                nc.vector.tensor_tensor(out=res[h][:, cols], in0=acc_p[:], in1=gates[h][:, cols], op=ALU.mult)
+        for h, queue in enumerate((nc.sync, nc.scalar)):
+            queue.dma_start(out=out[h * P : (h + 1) * P, :], in_=res[h][:])

@@ -20,8 +20,8 @@ PACK = 4
 FLOPS = 2 * (4 * K * R * J + R * N * O)
 
 
-def load_scale_rows(queue, plane, scales):
-    for q in range(4):
+def load_scale_rows(queue, plane, scales, quadrants):
+    for q in quadrants:
         queue.dma_start(
             out=plane[32 * q : 32 * q + 4, :].bitcast(I32),
             in_=scales[0, 4 * q : 4 * q + 4, :].bitcast(I32),
@@ -50,116 +50,125 @@ def tile_list_crossed_shared_one_finalgate_kernel(
         xo_sc = new([P, Z], U8, "xo_sc")
         w_sc_raw = new([P, R], U8, "w_sc_raw")
         w2_sc_raw = new([P, R], U8, "w2_sc_raw")
-        nc.gpsimd.memset(w2_sc_raw[:].bitcast(I32), 0)
-        for plane in (xt_sc, xo_sc, w_sc_raw):
+        wb_sc = new([P, N], U8, "wb_sc")
+        nc.gpsimd.memset(w_sc_raw[:].bitcast(I32), 0)
+        for plane in (xt_sc, xo_sc, w2_sc_raw, wb_sc):
             nc.vector.memset(plane[:].bitcast(I32), 0)
+
+        warm_in = new([P, 1], F32, "warm_in")
+        warm_out = new([P, 1], F32, "warm_out")
+        nc.gpsimd.memset(warm_in[:], 0.0)
+        nc.scalar.activation(out=warm_out[:], in_=warm_in[:], func=ACT.Sigmoid)
 
         xt_tab = new([P, T], U16, "xt_tab")
         xo_tab = new([P, Z], U32, "xo_tab")
         w_raw = new([P, R], U32, "w_raw")
         w2_raw = new([P, R], U32, "w2_raw")
+        wb_codes = new([P, 2 * N], U8, "wb_codes")
+        tz_tab = [new([P, E], F32, "tz%d" % h) for h in range(2)]
+        slope = new([P, 2], F32, "slope")
+        offset = new([P, 2], F32, "offset")
+
+        def load_words(tile, words):
+            nc.sync.dma_start(out=tile[:].bitcast(I32), in_=words[0].rearrange("p n t -> p (n t)").bitcast(I32))
 
         nc.sync.dma_start(l_xt[:], offs)
         nc.sync.dma_start(l_xo[:], offs2)
+        load_scale_rows(nc.gpsimd, w_sc_raw, w_scales, range(3))
+        load_scale_rows(nc.sync, xt_sc, xt_scales, range(4))
         nc.sync.dma_start(out=xt_tab[:].bitcast(I32), in_=xt_words[0].bitcast(I32))
-        load_scale_rows(nc.sync, xt_sc, xt_scales)
-        nc.sync.dma_start(out=xo_tab[:].bitcast(I32), in_=xo_words[0].rearrange("p n t -> p (n t)").bitcast(I32))
-        load_scale_rows(nc.sync, xo_sc, xo_scales)
-        nc.sync.dma_start(out=w_raw[:].bitcast(I32), in_=w_words[0].rearrange("p n t -> p (n t)").bitcast(I32))
-        nc.sync.dma_start(out=w2_raw[:].bitcast(I32), in_=w2_words[0].rearrange("p n t -> p (n t)").bitcast(I32))
-        load_scale_rows(nc.sync, w_sc_raw, w_scales)
-        load_scale_rows(nc.gpsimd, w2_sc_raw, w2_scales)
+        load_words(w_raw, w_words)
+        load_scale_rows(nc.sync, xo_sc, xo_scales, range(4))
+        load_words(xo_tab, xo_words)
+        load_words(w2_raw, w2_words)
+        load_scale_rows(nc.sync, w_sc_raw, w_scales, range(3, 4))
+        load_scale_rows(nc.sync, w2_sc_raw, w2_scales, range(4))
         nc.sync.dma_start(l_a[:], offs3)
         nc.sync.dma_start(l_b[:], offs4)
         nc.sync.dma_start(l_hid[:], offs5)
         nc.sync.dma_start(l_gate[:], offs6)
-
-        pw = [new([P, C], F32, "pw%d" % t) for t in range(2)]
-        pv = [new([P, C], F32, "pv%d" % t) for t in range(2)]
-        for t in range(2):
-            nc.vector.memset(pw[t][:], 0.0)
-            nc.vector.memset(pv[t][:], 0.0)
-
-        xt_g = new([P, J], U16, "xt_g")
-        xt_gs = new([P, J], U8, "xt_gs")
-        xo_g = new([P, J], U32, "xo_g")
-        xo_gs = new([P, J], U8, "xo_gs")
-        w_codes = new([P, R], U32, "w_codes")
-        w2_codes = new([P, R], U32, "w2_codes")
-        w_sc = new([P, R], U8, "w_sc")
-        w2_sc = new([P, R], U8, "w2_sc")
-
-        nc.vector.tensor_copy(out=xt_g[:], in_=xt_tab[:].indirect(l_xt[:]))
-        nc.vector.tensor_copy(out=xt_gs[:], in_=xt_sc[:].indirect(l_xt[:]))
-        nc.vector.tensor_copy(out=xo_g[:], in_=xo_tab[:].indirect(l_xo[:]))
-        nc.vector.tensor_copy(out=xo_gs[:], in_=xo_sc[:].indirect(l_xo[:]))
-        for dst, raw in ((w_codes, w_raw), (w2_codes, w2_raw)):
-            nc.scalar.copy(
-                out=dst[:].rearrange("p (t g i) -> p g t i", t=PACK, i=4),
-                in_=raw[:].rearrange("p (g i t) -> p g t i", t=PACK, i=4),
-            )
-        for dst, raw in ((w_sc, w_sc_raw), (w2_sc, w2_sc_raw)):
-            nc.vector.tensor_copy(
-                out=dst[:].rearrange("p (t g i) -> p g t i", t=PACK, i=16),
-                in_=raw[:].rearrange("p (g i t) -> p g t i", t=PACK, i=16),
-            )
-
-        tz_tab = [new([P, E], F32, "tz%d" % h, tag) for h, tag in enumerate(("xt_tab", "xo_tab"))]
-        slope = new([P, 2], F32, "slope", "xt_sc")
-        offset = new([P, 2], F32, "offset", "xo_sc")
-        wb_codes = new([P, 2 * N], U8, "wb_codes", "w_raw")
-        wb_sc = new([P, N], U8, "wb_sc", "w2_sc_raw")
-        nc.gpsimd.memset(wb_sc[:].bitcast(I32), 0)
-        nc.sync.dma_start(out=wb_codes[:].bitcast(I32), in_=wb_words[0].bitcast(I32))
-        load_scale_rows(nc.sync, wb_sc, wb_scales)
         for h in range(2):
             nc.sync.dma_start(out=tz_tab[h][:], in_=tz[h * P : (h + 1) * P, :])
         with nc.allow_non_contiguous_dma(reason="one slope and one offset a partition"):
             nc.sync.dma_start(out=slope[:], in_=so.rearrange("(h p) o -> p (h o)", p=P))
             nc.sync.dma_start(out=offset[:], in_=bo.rearrange("(h p) o -> p (h o)", p=P))
+        nc.sync.dma_start(out=wb_codes[:].bitcast(I32), in_=wb_words[0].bitcast(I32))
+        load_scale_rows(nc.sync, wb_sc, wb_scales, range(4))
 
-        def product(acc, t, first, first_sc, first_fmt, second, second_sc, second_fmt):
-            cols = slice(t * P, (t + 1) * P)
+        pw = [new([P, C], F32, "pw%d" % i) for i in range(2)]
+        pv = [new([P, C], F32, "pv%d" % i) for i in range(2)]
+        for i in range(2):
+            nc.vector.memset(pw[i][:], 0.0)
+            nc.vector.memset(pv[i][:], 0.0)
+
+        xt_g = new([P, J], U16, "xt_g")
+        xt_gs = new([P, J], U8, "xt_gs")
+        xo_g = new([P, J], U32, "xo_g")
+        xo_gs = new([P, J], U8, "xo_gs")
+        nc.vector.tensor_copy(out=xt_gs[:], in_=xt_sc[:].indirect(l_xt[:]))
+        nc.vector.tensor_copy(out=xt_g[:], in_=xt_tab[:].indirect(l_xt[:]))
+        nc.vector.tensor_copy(out=xo_gs[:], in_=xo_sc[:].indirect(l_xo[:]))
+        nc.vector.tensor_copy(out=xo_g[:], in_=xo_tab[:].indirect(l_xo[:]))
+
+        def deal(copy, raw, dtype, name, line):
+            first = new([P, P], dtype, name + "_first")
+            rest = new([P, (PACK - 1) * P], dtype, name + "_rest")
+            by_t = raw[:].rearrange("p (g i t) -> p g t i", t=PACK, i=line)
+            copy(out=first[:].rearrange("p (g i) -> p g i", i=line), in_=by_t[:, :, 0, :])
+            copy(out=rest[:].rearrange("p (t g i) -> p g t i", t=PACK - 1, i=line), in_=by_t[:, :, 1:PACK, :])
+            return [first[:]] + [rest[:, t * P : (t + 1) * P] for t in range(PACK - 1)]
+
+        w_codes = deal(nc.scalar.copy, w_raw, U32, "w_codes", 4)
+        w2_codes = deal(nc.scalar.copy, w2_raw, U32, "w2_codes", 4)
+        w_sc = deal(nc.gpsimd.tensor_copy, w_sc_raw, U8, "w_sc", 16)
+        w2_sc = deal(nc.vector.tensor_copy, w2_sc_raw, U8, "w2_sc", 16)
+
+        xt_op = (xt_g[:].bitcast(E2M1), xt_gs[:])
+        xo_op = (xo_g[:].bitcast(E4M3), xo_gs[:])
+
+        def product(acc, t, with_w2, with_w):
             nc.tensor.matmul_mx(
-                out=acc[:], lhsT=first[:, cols].bitcast(first_fmt), lhsT_scale=first_sc[:, cols],
-                rhs=xt_g[:].bitcast(E2M1), rhs_scale=xt_gs[:], start=True, stop=False,
+                out=acc[:], lhsT=w2_codes[t].bitcast(E5M2), lhsT_scale=w2_sc[t],
+                rhs=with_w2[0], rhs_scale=with_w2[1], start=True, stop=False,
             )
             nc.tensor.matmul_mx(
-                out=acc[:], lhsT=second[:, cols].bitcast(second_fmt), lhsT_scale=second_sc[:, cols],
-                rhs=xo_g[:].bitcast(E4M3), rhs_scale=xo_gs[:], start=False, stop=True,
+                out=acc[:], lhsT=w_codes[t].bitcast(E4M3), lhsT_scale=w_sc[t],
+                rhs=with_w[0], rhs_scale=with_w[1], start=False, stop=True,
             )
 
         hid_planes = new([P, PACK, O], BF16, "hid_planes")
         half = O // 2
         for t in range(PACK):
-            acc_a = ps.tile([P, J], F32, name="acc_a", tag="acc_a%d" % (t % 3))
-            acc_b = ps.tile([P, J], F32, name="acc_b", tag="acc_b%d" % (t % 3))
-            product(acc_a, t, w_codes, w_sc, E4M3, w2_codes, w2_sc, E5M2)
-            product(acc_b, t, w2_codes, w2_sc, E5M2, w_codes, w_sc, E4M3)
-            a_sb = sb.tile([P, J], F32, name="a_sb", tag="a_sb%d" % t, align_bytes=64)
-            b_sb = sb.tile([P, J], F32, name="b_sb", tag="b_sb%d" % t, align_bytes=64)
+            acc_a = ps.tile([P, J], F32, name="acc_a", tag="acc_a%d" % (t == 2))
+            acc_b = ps.tile([P, J], F32, name="acc_b", tag="acc_b%d" % (t == 2))
+            product(acc_a, t, xo_op, xt_op)
+            product(acc_b, t, xt_op, xo_op)
+            a_sb = new([P, J], F32, "a_sb%d" % t)
+            b_sb = new([P, J], F32, "b_sb%d" % t)
             nc.scalar.copy(out=a_sb[:], in_=acc_a[:])
             nc.vector.tensor_copy(out=b_sb[:], in_=acc_b[:])
             nc.scalar.activation(out=pw[t % 2][:].indirect(l_a[:]), in_=a_sb[:], func=ACT.Copy)
             nc.vector.tensor_copy(out=pv[t % 2][:].indirect(l_b[:]), in_=b_sb[:])
-            pg = sb.tile([P, C], F32, name="pg", tag="pg%d" % t, align_bytes=64)
-            nc.vector.tensor_tensor(out=pg[:], in0=pw[t % 2][:], in1=pv[t % 2][:], op=ALU.add)
-            if t < PACK - 1:
+            pg = new([P, C], F32, "pg%d" % t)
+            adder = nc.gpsimd if t in [0,1,2] else nc.vector
+            adder.tensor_tensor(out=pg[:], in0=pw[t % 2][:], in1=pv[t % 2][:], op=ALU.add)
+            if t in [0]:
+                nc.vector.tensor_copy(out=hid_planes[:, t, :], in_=pg[:].indirect(l_hid[:]))
+            elif t < PACK - 1:
                 nc.scalar.activation(out=hid_planes[:, t, :], in_=pg[:].indirect(l_hid[:]), func=ACT.Copy)
             else:
                 nc.vector.tensor_copy(out=hid_planes[:, t, 0:half], in_=pg[:].indirect(l_hid[:, 0:8]))
                 nc.scalar.activation(out=hid_planes[:, t, half:O], in_=pg[:].indirect(l_hid[:, 8:16]), func=ACT.Copy)
 
         def make_gate(h, tag):
-            gate = sb.tile([P, O], F32, name="gate", tag=tag, align_bytes=64)
+            gate = new([P, O], F32, "gate%d" % h, tag)
             nc.scalar.activation(
                 out=gate[:], in_=tz_tab[h][:].indirect(l_gate[:]), func=ACT.Sigmoid,
                 bias=offset[:, h : h + 1], scale=slope[:, h : h + 1],
             )
             return gate
 
-        gates = [make_gate(0, "a_sb3")]
-
+        gates = [make_gate(0, "a_sb1")]
         hid_words = [new([P, half * PACK], BF16, "hid_words%d" % u) for u in range(2)]
         for u, copy in enumerate((nc.vector.tensor_copy, nc.scalar.copy)):
             copy(
@@ -167,19 +176,19 @@ def tile_list_crossed_shared_one_finalgate_kernel(
                 in_=hid_planes[:, :, u * half : (u + 1) * half].rearrange("p t (c i) -> p c t i", i=4),
             )
         gates.append(make_gate(1, "pg3"))
-        res = [new([P, O], F32, "res%d" % h) for h in range(2)]
+        hid_codes = [new([P, half], U32, "hid_codes%d" % u) for u in range(2)]
+        hid_sc = [new([P, half], U8, "hid_sc%d" % u) for u in range(2)]
         for u in range(2):
-            cols = slice(u * half, (u + 1) * half)
-            hid_codes = new([P, half], U32, "hid_codes%d" % u)
-            hid_sc = new([P, half], U8, "hid_sc%d" % u)
-            nc.vector.quantize_mx(out=hid_codes[:].bitcast(E5M2), scales=hid_sc[:], in_=hid_words[u][:])
-            for h in range(2):
-                acc_p = ps.tile([P, half], F32, name="acc_p", tag=("acc_p0", "acc_p1", "acc_a1", "acc_b1")[2 * u + h])
-                nc.tensor.matmul_mx(
-                    out=acc_p[:], lhsT=wb_codes[:, 2 * h * P : 2 * (h + 1) * P].bitcast(E2M1),
-                    lhsT_scale=wb_sc[:, h * P : (h + 1) * P],
-                    rhs=hid_codes[:].bitcast(E5M2), rhs_scale=hid_sc[:], start=True, stop=True,
-                )
-                nc.vector.tensor_tensor(out=res[h][:, cols], in0=acc_p[:], in1=gates[h][:, cols], op=ALU.mult)
+            nc.vector.quantize_mx(out=hid_codes[u][:].bitcast(E5M2), scales=hid_sc[u][:], in_=hid_words[u][:])
         for h, queue in enumerate((nc.sync, nc.scalar)):
-            queue.dma_start(out=out[h * P : (h + 1) * P, :], in_=res[h][:])
+            acc_p = ps.tile([P, O], F32, name="acc_p", tag="acc_p%d" % h)
+            for u in range(2):
+                nc.tensor.matmul_mx(
+                    out=acc_p[:, u * half : (u + 1) * half],
+                    lhsT=wb_codes[:, 2 * h * P : 2 * (h + 1) * P].bitcast(E2M1),
+                    lhsT_scale=wb_sc[:, h * P : (h + 1) * P],
+                    rhs=hid_codes[u][:].bitcast(E5M2), rhs_scale=hid_sc[u][:], start=True, stop=True,
+                )
+            res = new([P, O], F32, "res%d" % h)
+            nc.vector.tensor_tensor(out=res[:], in0=acc_p[:], in1=gates[h][:], op=ALU.mult)
+            queue.dma_start(out=out[h * P : (h + 1) * P, :], in_=res[:])

@@ -17,15 +17,15 @@ ALU = mybir.AluOpType
 K, T, Z, J, R, C, O, N, E = 512, 1024, 1024, 256, 512, 512, 256, 256, 1024
 P = 128
 PACK = 4
+LAST = PACK - 1
+HALF = O // 2
+LIST_COLS = J // 16
 FLOPS = 2 * (4 * K * R * J + R * N * O)
 
 
-def load_scale_rows(queue, plane, scales, quadrants):
-    for q in quadrants:
-        queue.dma_start(
-            out=plane[32 * q : 32 * q + 4, :].bitcast(I32),
-            in_=scales[0, 4 * q : 4 * q + 4, :].bitcast(I32),
-        )
+def load_scale_rows(queue, plane, scales, rows):
+    for s in rows:
+        queue.dma_start(out=plane[s:P:32, :].bitcast(I32), in_=scales[0, s:16:4, :].bitcast(I32))
 
 
 def tile_list_crossed_shared_one_finalgate_kernel(
@@ -38,13 +38,12 @@ def tile_list_crossed_shared_one_finalgate_kernel(
         sb = ctx.enter_context(tc.tile_pool(name="sb", bufs=1))
         ps = ctx.enter_context(tc.psum_pool(name="ps", bufs=1))
 
-        def new_list(name):
-            return lists.tile([P, J // 16], U16, name=name)
-
         def new(shape, dtype, name, tag=None):
             return sb.tile(shape, dtype, name=name, tag=tag or name, align_bytes=64)
 
-        l_xt, l_xo, l_a, l_b, l_hid, l_gate = [new_list("list%d" % i) for i in range(6)]
+        l_xt, l_xo, l_a, l_b, l_hid, l_gate = [
+            lists.tile([P, LIST_COLS], U16, name="list%d" % i) for i in range(6)
+        ]
 
         xt_sc = new([P, T], U8, "xt_sc")
         xo_sc = new([P, Z], U8, "xo_sc")
@@ -79,9 +78,9 @@ def tile_list_crossed_shared_one_finalgate_kernel(
         nc.sync.dma_start(out=xt_tab[:].bitcast(I32), in_=xt_words[0].bitcast(I32))
         load_words(w_raw, w_words)
         load_scale_rows(nc.sync, xo_sc, xo_scales, range(4))
+        load_scale_rows(nc.sync, w_sc_raw, w_scales, range(3, 4))
         load_words(xo_tab, xo_words)
         load_words(w2_raw, w2_words)
-        load_scale_rows(nc.sync, w_sc_raw, w_scales, range(3, 4))
         load_scale_rows(nc.sync, w2_sc_raw, w2_scales, range(4))
         nc.sync.dma_start(l_a[:], offs3)
         nc.sync.dma_start(l_b[:], offs4)
@@ -97,9 +96,11 @@ def tile_list_crossed_shared_one_finalgate_kernel(
 
         pw = [new([P, C], F32, "pw%d" % i) for i in range(2)]
         pv = [new([P, C], F32, "pv%d" % i) for i in range(2)]
+        odd = C // 2 - 1
         for i in range(2):
-            nc.vector.memset(pw[i][:], 0.0)
-            nc.vector.memset(pv[i][:], 0.0)
+            for board in (pw[i], pv[i]):
+                nc.vector.memset(board[:, 0:odd], 0.0)
+                nc.vector.memset(board[:, odd:C], 0.0)
 
         xt_g = new([P, J], U16, "xt_g")
         xt_gs = new([P, J], U8, "xt_gs")
@@ -112,11 +113,11 @@ def tile_list_crossed_shared_one_finalgate_kernel(
 
         def deal(copy, raw, dtype, name, line):
             first = new([P, P], dtype, name + "_first")
-            rest = new([P, (PACK - 1) * P], dtype, name + "_rest")
+            rest = new([P, LAST * P], dtype, name + "_rest")
             by_t = raw[:].rearrange("p (g i t) -> p g t i", t=PACK, i=line)
             copy(out=first[:].rearrange("p (g i) -> p g i", i=line), in_=by_t[:, :, 0, :])
-            copy(out=rest[:].rearrange("p (t g i) -> p g t i", t=PACK - 1, i=line), in_=by_t[:, :, 1:PACK, :])
-            return [first[:]] + [rest[:, t * P : (t + 1) * P] for t in range(PACK - 1)]
+            copy(out=rest[:].rearrange("p (t g i) -> p g t i", t=LAST, i=line), in_=by_t[:, :, 1:PACK, :])
+            return [first[:]] + [rest[:, t * P : (t + 1) * P] for t in range(LAST)]
 
         w_codes = deal(nc.scalar.copy, w_raw, U32, "w_codes", 4)
         w2_codes = deal(nc.scalar.copy, w2_raw, U32, "w2_codes", 4)
@@ -126,23 +127,26 @@ def tile_list_crossed_shared_one_finalgate_kernel(
         xt_op = (xt_g[:].bitcast(E2M1), xt_gs[:])
         xo_op = (xo_g[:].bitcast(E4M3), xo_gs[:])
 
-        def product(acc, t, with_w2, with_w):
-            nc.tensor.matmul_mx(
-                out=acc[:], lhsT=w2_codes[t].bitcast(E5M2), lhsT_scale=w2_sc[t],
-                rhs=with_w2[0], rhs_scale=with_w2[1], start=True, stop=False,
-            )
-            nc.tensor.matmul_mx(
-                out=acc[:], lhsT=w_codes[t].bitcast(E4M3), lhsT_scale=w_sc[t],
-                rhs=with_w[0], rhs_scale=with_w[1], start=False, stop=True,
-            )
+        def product(acc, t, with_w, with_w2):
+            passes = [
+                (w_codes[t].bitcast(E4M3), w_sc[t], with_w),
+                (w2_codes[t].bitcast(E5M2), w2_sc[t], with_w2),
+            ]
+            if t > 0:
+                passes = passes[::-1]
+            for i, (codes, scales, moving) in enumerate(passes):
+                nc.tensor.matmul_mx(
+                    out=acc[:], lhsT=codes, lhsT_scale=scales,
+                    rhs=moving[0], rhs_scale=moving[1], start=(i == 0), stop=(i == 1),
+                )
 
+        bank_of_slice = (0, 0, 1, 0)
         hid_planes = new([P, PACK, O], BF16, "hid_planes")
-        half = O // 2
         for t in range(PACK):
-            acc_a = ps.tile([P, J], F32, name="acc_a", tag="acc_a%d" % (t == 2))
-            acc_b = ps.tile([P, J], F32, name="acc_b", tag="acc_b%d" % (t == 2))
-            product(acc_a, t, xo_op, xt_op)
-            product(acc_b, t, xt_op, xo_op)
+            acc_a = ps.tile([P, J], F32, name="acc_a", tag="acc_a%d" % bank_of_slice[t])
+            acc_b = ps.tile([P, J], F32, name="acc_b", tag="acc_b%d" % bank_of_slice[t])
+            product(acc_a, t, xt_op, xo_op)
+            product(acc_b, t, xo_op, xt_op)
             a_sb = new([P, J], F32, "a_sb%d" % t)
             b_sb = new([P, J], F32, "b_sb%d" % t)
             nc.scalar.copy(out=a_sb[:], in_=acc_a[:])
@@ -150,15 +154,16 @@ def tile_list_crossed_shared_one_finalgate_kernel(
             nc.scalar.activation(out=pw[t % 2][:].indirect(l_a[:]), in_=a_sb[:], func=ACT.Copy)
             nc.vector.tensor_copy(out=pv[t % 2][:].indirect(l_b[:]), in_=b_sb[:])
             pg = new([P, C], F32, "pg%d" % t)
-            adder = nc.gpsimd if t in [0,1,2] else nc.vector
+            adder = nc.vector if t == LAST else nc.gpsimd
             adder.tensor_tensor(out=pg[:], in0=pw[t % 2][:], in1=pv[t % 2][:], op=ALU.add)
-            if t in [0]:
+            if t == 0:
                 nc.vector.tensor_copy(out=hid_planes[:, t, :], in_=pg[:].indirect(l_hid[:]))
-            elif t < PACK - 1:
+            elif t < LAST:
                 nc.scalar.activation(out=hid_planes[:, t, :], in_=pg[:].indirect(l_hid[:]), func=ACT.Copy)
             else:
-                nc.vector.tensor_copy(out=hid_planes[:, t, 0:half], in_=pg[:].indirect(l_hid[:, 0:8]))
-                nc.scalar.activation(out=hid_planes[:, t, half:O], in_=pg[:].indirect(l_hid[:, 8:16]), func=ACT.Copy)
+                lo, hi = l_hid[:, 0 : LIST_COLS // 2], l_hid[:, LIST_COLS // 2 : LIST_COLS]
+                nc.vector.tensor_copy(out=hid_planes[:, t, 0:HALF], in_=pg[:].indirect(lo))
+                nc.scalar.activation(out=hid_planes[:, t, HALF:O], in_=pg[:].indirect(hi), func=ACT.Copy)
 
         def make_gate(h, tag):
             gate = new([P, O], F32, "gate%d" % h, tag)
@@ -169,22 +174,23 @@ def tile_list_crossed_shared_one_finalgate_kernel(
             return gate
 
         gates = [make_gate(0, "a_sb1")]
-        hid_words = [new([P, half * PACK], BF16, "hid_words%d" % u) for u in range(2)]
+        hid_words = [new([P, HALF * PACK], BF16, "hid_words%d" % u) for u in range(2)]
         for u, copy in enumerate((nc.vector.tensor_copy, nc.scalar.copy)):
             copy(
                 out=hid_words[u][:].rearrange("p (c i t) -> p c t i", t=PACK, i=4),
-                in_=hid_planes[:, :, u * half : (u + 1) * half].rearrange("p t (c i) -> p c t i", i=4),
+                in_=hid_planes[:, :, u * HALF : (u + 1) * HALF].rearrange("p t (c i) -> p c t i", i=4),
             )
-        gates.append(make_gate(1, "pg3"))
-        hid_codes = [new([P, half], U32, "hid_codes%d" % u) for u in range(2)]
-        hid_sc = [new([P, half], U8, "hid_sc%d" % u) for u in range(2)]
+        gates.append(make_gate(1, "pg%d" % LAST))
+        hid_codes = [new([P, HALF], U32, "hid_codes%d" % u) for u in range(2)]
+        hid_sc = [new([P, HALF], U8, "hid_sc%d" % u) for u in range(2)]
         for u in range(2):
             nc.vector.quantize_mx(out=hid_codes[u][:].bitcast(E5M2), scales=hid_sc[u][:], in_=hid_words[u][:])
+
         for h, queue in enumerate((nc.sync, nc.scalar)):
             acc_p = ps.tile([P, O], F32, name="acc_p", tag="acc_p%d" % h)
             for u in range(2):
                 nc.tensor.matmul_mx(
-                    out=acc_p[:, u * half : (u + 1) * half],
+                    out=acc_p[:, u * HALF : (u + 1) * HALF],
                     lhsT=wb_codes[:, 2 * h * P : 2 * (h + 1) * P].bitcast(E2M1),
                     lhsT_scale=wb_sc[:, h * P : (h + 1) * P],
                     rhs=hid_codes[u][:].bitcast(E5M2), rhs_scale=hid_sc[u][:], start=True, stop=True,

from contextlib import ExitStack

import concourse.mybir as mybir

F32 = mybir.dt.float32
BF16 = mybir.dt.bfloat16
I32 = mybir.dt.int32
U32 = mybir.dt.uint32
U16 = mybir.dt.uint16
U8 = mybir.dt.uint8
E4M3 = mybir.dt.float8_e4m3fn_x4
E5M2 = mybir.dt.float8_e5m2_x4
E2M1 = mybir.dt.float4_e2m1fn_x4
ACT = mybir.ActivationFunctionType
ALU = mybir.AluOpType

K, T, Z, J, R, C, O, N, E = 512, 1024, 1024, 256, 512, 512, 256, 256, 1024
P = 128
PACK = 4
LAST = PACK - 1
HALF = O // 2
LIST_COLS = J // 16
FLOPS = 2 * (4 * K * R * J + R * N * O)


def load_scale_rows(queue, plane, scales, rows):
    for s in rows:
        queue.dma_start(out=plane[s:P:32, :].bitcast(I32), in_=scales[0, s:16:4, :].bitcast(I32))


def tile_list_crossed_shared_one_finalgate_kernel(
    tc, xt_words, xt_scales, xo_words, xo_scales, w_words, w_scales, w2_words, w2_scales,
    wb_words, wb_scales, tz, so, bo, offs, offs2, offs3, offs4, offs5, offs6, out,
):
    nc = tc.nc
    with ExitStack() as ctx:
        lists = ctx.enter_context(tc.tile_pool(name="lists", bufs=1))
        sb = ctx.enter_context(tc.tile_pool(name="sb", bufs=1))
        ps = ctx.enter_context(tc.psum_pool(name="ps", bufs=1))

        def new(shape, dtype, name, tag=None):
            return sb.tile(shape, dtype, name=name, tag=tag or name, align_bytes=64)

        l_xt, l_xo, l_a, l_b, l_hid, l_gate = [
            lists.tile([P, LIST_COLS], U16, name="list%d" % i) for i in range(6)
        ]

        xt_sc = new([P, T], U8, "xt_sc")
        xo_sc = new([P, Z], U8, "xo_sc")
        w_sc_raw = new([P, R], U8, "w_sc_raw")
        w2_sc_raw = new([P, R], U8, "w2_sc_raw")
        wb_sc = new([P, N], U8, "wb_sc")
        nc.gpsimd.memset(w_sc_raw[:].bitcast(I32), 0)
        for plane in (xt_sc, xo_sc, w2_sc_raw, wb_sc):
            nc.vector.memset(plane[:].bitcast(I32), 0)

        warm_in = new([P, 1], F32, "warm_in")
        warm_out = new([P, 1], F32, "warm_out")
        nc.gpsimd.memset(warm_in[:], 0.0)
        nc.scalar.activation(out=warm_out[:], in_=warm_in[:], func=ACT.Sigmoid)

        xt_tab = new([P, T], U16, "xt_tab")
        xo_tab = new([P, Z], U32, "xo_tab")
        w_raw = new([P, R], U32, "w_raw")
        w2_raw = new([P, R], U32, "w2_raw")
        wb_codes = new([P, 2 * N], U8, "wb_codes")
        tz_tab = [new([P, E], F32, "tz%d" % h) for h in range(2)]
        slope = new([P, 2], F32, "slope")
        offset = new([P, 2], F32, "offset")

        def load_words(tile, words):
            nc.sync.dma_start(out=tile[:].bitcast(I32), in_=words[0].rearrange("p n t -> p (n t)").bitcast(I32))

        nc.sync.dma_start(l_xt[:], offs)
        nc.sync.dma_start(l_xo[:], offs2)
        load_scale_rows(nc.gpsimd, w_sc_raw, w_scales, range(3))
        load_scale_rows(nc.sync, xt_sc, xt_scales, range(4))
        nc.sync.dma_start(out=xt_tab[:].bitcast(I32), in_=xt_words[0].bitcast(I32))
        load_words(w_raw, w_words)
        load_scale_rows(nc.sync, xo_sc, xo_scales, range(4))
        load_scale_rows(nc.sync, w_sc_raw, w_scales, range(3, 4))
        load_words(xo_tab, xo_words)
        load_words(w2_raw, w2_words)
        load_scale_rows(nc.sync, w2_sc_raw, w2_scales, range(4))
        nc.sync.dma_start(l_a[:], offs3)
        nc.sync.dma_start(l_b[:], offs4)
        nc.sync.dma_start(l_hid[:], offs5)
        nc.sync.dma_start(l_gate[:], offs6)
        for h in range(2):
            nc.sync.dma_start(out=tz_tab[h][:], in_=tz[h * P : (h + 1) * P, :])
        with nc.allow_non_contiguous_dma(reason="one slope and one offset a partition"):
            nc.sync.dma_start(out=slope[:], in_=so.rearrange("(h p) o -> p (h o)", p=P))
            nc.sync.dma_start(out=offset[:], in_=bo.rearrange("(h p) o -> p (h o)", p=P))
        nc.sync.dma_start(out=wb_codes[:].bitcast(I32), in_=wb_words[0].bitcast(I32))
        load_scale_rows(nc.sync, wb_sc, wb_scales, range(4))

        pw = [new([P, C], F32, "pw%d" % i) for i in range(2)]
        pv = [new([P, C], F32, "pv%d" % i) for i in range(2)]
        odd = C // 2 - 1
        for i in range(2):
            for board in (pw[i], pv[i]):
                nc.vector.memset(board[:, 0:odd], 0.0)
                nc.vector.memset(board[:, odd:C], 0.0)

        xt_g = new([P, J], U16, "xt_g")
        xt_gs = new([P, J], U8, "xt_gs")
        xo_g = new([P, J], U32, "xo_g")
        xo_gs = new([P, J], U8, "xo_gs")
        nc.vector.tensor_copy(out=xt_gs[:], in_=xt_sc[:].indirect(l_xt[:]))
        nc.vector.tensor_copy(out=xt_g[:], in_=xt_tab[:].indirect(l_xt[:]))
        nc.vector.tensor_copy(out=xo_gs[:], in_=xo_sc[:].indirect(l_xo[:]))
        nc.vector.tensor_copy(out=xo_g[:], in_=xo_tab[:].indirect(l_xo[:]))

        def deal(copy, raw, dtype, name, line):
            first = new([P, P], dtype, name + "_first")
            rest = new([P, LAST * P], dtype, name + "_rest")
            by_t = raw[:].rearrange("p (g i t) -> p g t i", t=PACK, i=line)
            copy(out=first[:].rearrange("p (g i) -> p g i", i=line), in_=by_t[:, :, 0, :])
            copy(out=rest[:].rearrange("p (t g i) -> p g t i", t=LAST, i=line), in_=by_t[:, :, 1:PACK, :])
            return [first[:]] + [rest[:, t * P : (t + 1) * P] for t in range(LAST)]

        w_codes = deal(nc.scalar.copy, w_raw, U32, "w_codes", 4)
        w2_codes = deal(nc.scalar.copy, w2_raw, U32, "w2_codes", 4)
        w_sc = deal(nc.gpsimd.tensor_copy, w_sc_raw, U8, "w_sc", 16)
        w2_sc = deal(nc.vector.tensor_copy, w2_sc_raw, U8, "w2_sc", 16)

        xt_op = (xt_g[:].bitcast(E2M1), xt_gs[:])
        xo_op = (xo_g[:].bitcast(E4M3), xo_gs[:])

        def product(acc, t, with_w, with_w2):
            passes = [
                (w_codes[t].bitcast(E4M3), w_sc[t], with_w),
                (w2_codes[t].bitcast(E5M2), w2_sc[t], with_w2),
            ]
            if t > 0:
                passes = passes[::-1]
            for i, (codes, scales, moving) in enumerate(passes):
                nc.tensor.matmul_mx(
                    out=acc[:], lhsT=codes, lhsT_scale=scales,
                    rhs=moving[0], rhs_scale=moving[1], start=(i == 0), stop=(i == 1),
                )

        bank_of_slice = (0, 0, 1, 0)
        hid_planes = new([P, PACK, O], BF16, "hid_planes")
        for t in range(PACK):
            acc_a = ps.tile([P, J], F32, name="acc_a", tag="acc_a%d" % bank_of_slice[t])
            acc_b = ps.tile([P, J], F32, name="acc_b", tag="acc_b%d" % bank_of_slice[t])
            product(acc_a, t, xt_op, xo_op)
            product(acc_b, t, xo_op, xt_op)
            a_sb = new([P, J], F32, "a_sb%d" % t)
            b_sb = new([P, J], F32, "b_sb%d" % t)
            nc.scalar.copy(out=a_sb[:], in_=acc_a[:])
            nc.vector.tensor_copy(out=b_sb[:], in_=acc_b[:])
            nc.scalar.activation(out=pw[t % 2][:].indirect(l_a[:]), in_=a_sb[:], func=ACT.Copy)
            nc.vector.tensor_copy(out=pv[t % 2][:].indirect(l_b[:]), in_=b_sb[:])
            pg = new([P, C], F32, "pg%d" % t)
            adder = nc.vector if t == LAST else nc.gpsimd
            adder.tensor_tensor(out=pg[:], in0=pw[t % 2][:], in1=pv[t % 2][:], op=ALU.add)
            if t == 0:
                nc.vector.tensor_copy(out=hid_planes[:, t, :], in_=pg[:].indirect(l_hid[:]))
            elif t < LAST:
                nc.scalar.activation(out=hid_planes[:, t, :], in_=pg[:].indirect(l_hid[:]), func=ACT.Copy)
            else:
                lo, hi = l_hid[:, 0 : LIST_COLS // 2], l_hid[:, LIST_COLS // 2 : LIST_COLS]
                nc.vector.tensor_copy(out=hid_planes[:, t, 0:HALF], in_=pg[:].indirect(lo))
                nc.scalar.activation(out=hid_planes[:, t, HALF:O], in_=pg[:].indirect(hi), func=ACT.Copy)

        def make_gate(h, tag):
            gate = new([P, O], F32, "gate%d" % h, tag)
            nc.scalar.activation(
                out=gate[:], in_=tz_tab[h][:].indirect(l_gate[:]), func=ACT.Sigmoid,
                bias=offset[:, h : h + 1], scale=slope[:, h : h + 1],
            )
            return gate

        gates = [make_gate(0, "a_sb1")]
        hid_words = [new([P, HALF * PACK], BF16, "hid_words%d" % u) for u in range(2)]
        for u, copy in enumerate((nc.vector.tensor_copy, nc.scalar.copy)):
            copy(
                out=hid_words[u][:].rearrange("p (c i t) -> p c t i", t=PACK, i=4),
                in_=hid_planes[:, :, u * HALF : (u + 1) * HALF].rearrange("p t (c i) -> p c t i", i=4),
            )
        gates.append(make_gate(1, "pg%d" % LAST))
        hid_codes = [new([P, HALF], U32, "hid_codes%d" % u) for u in range(2)]
        hid_sc = [new([P, HALF], U8, "hid_sc%d" % u) for u in range(2)]
        for u in range(2):
            nc.vector.quantize_mx(out=hid_codes[u][:].bitcast(E5M2), scales=hid_sc[u][:], in_=hid_words[u][:])

        for h, queue in enumerate((nc.sync, nc.scalar)):
            acc_p = ps.tile([P, O], F32, name="acc_p", tag="acc_p%d" % h)
            for u in range(2):
                nc.tensor.matmul_mx(
                    out=acc_p[:, u * HALF : (u + 1) * HALF],
                    lhsT=wb_codes[:, 2 * h * P : 2 * (h + 1) * P].bitcast(E2M1),
                    lhsT_scale=wb_sc[:, h * P : (h + 1) * P],
                    rhs=hid_codes[u][:].bitcast(E5M2), rhs_scale=hid_sc[u][:], start=True, stop=True,
                )
            res = new([P, O], F32, "res%d" % h)
            nc.vector.tensor_tensor(out=res[:], in0=acc_p[:], in1=gates[h][:], op=ALU.mult)
            queue.dma_start(out=out[h * P : (h + 1) * P, :], in_=res[:])
